import numpy as np
import ml_dtypes


def mxq(x, axis, fmt="e4m3"):
    dtype, down = {"e4m3": (ml_dtypes.float8_e4m3fn, 7), "e5m2": (ml_dtypes.float8_e5m2, 14)}[fmt]
    v = np.moveaxis(np.asarray(x, np.float32).astype(ml_dtypes.bfloat16).astype(np.float64), axis, -1)
    blocks = v.reshape(v.shape[:-1] + (-1, 32))
    amax = np.abs(blocks).max(-1, keepdims=True)
    byte = np.maximum(np.where(amax > 0, np.frexp(amax)[1] - 1 + 127, 0) - down, 1)
    scale = np.exp2(byte - 127.0)
    codes = (blocks / scale).astype(np.float32).astype(dtype).astype(np.float64)
    return np.moveaxis((codes * scale).reshape(v.shape), -1, axis)


WIDE = False


def mx_kscale(k):
    if not WIDE:
        return np.ones(k)
    levels = np.array([10, -10, 5, -5, 0])
    if k % 512:
        return np.exp2(np.random.permutation(np.resize(levels, k // 32))).repeat(32)
    a = np.empty((k // 512, 16))
    for p in range(k // 512):
        a[p, :8] = np.random.permutation(np.resize(levels, 8))
        for g in range(8):
            far = levels[np.abs(levels - a[p, g]) >= 10]
            a[p, g + 8] = far[np.random.randint(len(far))]
    return np.exp2(a.ravel()).repeat(32)


BF16 = ml_dtypes.bfloat16


def bf(x):
    return np.asarray(x, np.float32).astype(BF16)


def f64(x):
    return np.asarray(x).astype(np.float64)


E2M1 = np.array([0.0, 0.5, 1.0, 1.5, 2.0, 3.0, 4.0, 6.0, -0.0, -0.5, -1.0, -1.5, -2.0, -3.0, -4.0, -6.0])


def pack_weight(w, fmt):
    k, n = w.shape
    w = f64(bf(w)).reshape(k // 32, 32, n)
    amax = np.abs(w).max(1)
    if fmt == "e4m3":
        byte = np.frexp(amax)[1] - 1 + 127 - 7
    else:
        mant, ex = np.frexp(amax / 6.0)
        byte = np.where(mant > 0.5, ex, ex - 1) + 127
    byte = np.clip(np.where(amax > 0, byte, 1), 1, 254)
    scaled = (w * np.exp2(127.0 - byte)[:, None, :]).reshape(k, n).astype(np.float32)
    by_word = np.ascontiguousarray(scaled.reshape(k // 512, 128, 4, n).transpose(0, 1, 3, 2))
    if fmt == "e4m3":
        words = by_word.astype(ml_dtypes.float8_e4m3fn).view(np.uint8)
    else:
        c = by_word.astype(ml_dtypes.float4_e2m1fn).view(np.uint8) & 0xF
        words = c[..., 0::2] | (c[..., 1::2] << 4)
    return np.ascontiguousarray(words), np.ascontiguousarray(byte.astype(np.uint8).reshape(k // 512, 16, n))


def unpack_weight(words, scales, fmt):
    g, p, n, _ = words.shape
    if fmt == "e4m3":
        vals = np.ascontiguousarray(words).view(ml_dtypes.float8_e4m3fn).astype(np.float64)
    else:
        nib = np.empty((g, p, n, 4), np.uint8)
        nib[..., 0::2] = words & 0xF
        nib[..., 1::2] = words >> 4
        vals = E2M1[nib]
    vals = vals * np.repeat(np.exp2(scales.astype(np.float64) - 127.0), 8, axis=1)[..., None]
    return vals.transpose(0, 1, 3, 2).reshape(g * 512, n)
def pack4(w):
    words, scales = pack_weight(w, "e2m1")
    return words.reshape(words.shape[0], 128, -1), scales


def unpack4(words, scales):
    return unpack_weight(words.reshape(words.shape[0], 128, -1, 2), scales, "e2m1")


def planes(Y):
    n, m = Y.shape
    b = f64(bf(Y)).reshape(n // 32, 32, m)
    amax = np.abs(b).max(1)
    byte = np.clip(np.where(amax > 0, np.frexp(amax)[1] - 1 + 127 - 7, 1), 1, 254)
    codes = (b * np.exp2(127.0 - byte)[:, None, :]).reshape(n, m).astype(np.float32).astype(ml_dtypes.float8_e4m3fn).view(np.uint8)
    words = codes.reshape(n // 512, 128, 4, m).transpose(0, 1, 3, 2)
    return np.ascontiguousarray(words), np.ascontiguousarray(byte.astype(np.uint8).reshape(n // 512, 16, m))


T, K, F = 768, 1024, 1536

def setup_inputs():
    s = mx_kscale(K)[:, None]
    X = np.random.randn(K, T) * s
    U = np.random.randn(K, F) * 0.5 / np.sqrt(K) / s
    V = np.random.randn(K, F) * 0.5 / np.sqrt(K) / s
    size = np.exp(0.8 * np.random.randn(F))
    C = np.random.randn(K, F) / np.sqrt(K) * size / s
    x_words, x_scales = pack_weight(X, "e4m3")
    u_words, u_scales = pack4(U)
    v_words, v_scales = pack_weight(V, "e4m3")
    return {"x_words": x_words, "x_scales": x_scales,
            "u_words": u_words, "u_scales": u_scales,
            "v_words": v_words, "v_scales": v_scales,
            "colour": bf(C),
            "u_base": bf(1.0 + 0.1 * np.random.randn(F)),
            "v_base": bf(1.0 + 0.1 * np.random.randn(F))}

def reference(x_words, x_scales, u_words, u_scales, v_words, v_scales, colour, u_base, v_base):
    X = unpack_weight(x_words, x_scales, "e4m3")
    U = unpack4(u_words, u_scales)
    V = unpack_weight(v_words, v_scales, "e4m3")
    C = mxq(f64(colour), 0, "e4m3")
    first = X.T @ U
    second = X.T @ V
    basis = X.T @ C
    y = (first + f64(u_base)) * (second + f64(v_base)) * basis
    Y = y.T
    words, scales = planes(Y)
    return y, words, scales

@@ -1,0 +1,336 @@
+from contextlib import ExitStack
+
+import concourse.mybir as mybir
+from concourse.masks import make_identity
+
+T, K, F = 768, 1024, 1536
+FLOPS = 3 * 2 * T * K * F
+
+F32 = mybir.dt.float32
+BF16 = mybir.dt.bfloat16
+I32 = mybir.dt.int32
+U32 = mybir.dt.uint32
+U8 = mybir.dt.uint8
+FP8X4 = mybir.dt.float8_e4m3fn_x4
+FP4X4 = mybir.dt.float4_e2m1fn_x4
+ADD = mybir.AluOpType.add
+MULT = mybir.AluOpType.mult
+
+P = 128
+PASSES = 2
+CHUNK = 512
+CHUNKS = 3
+PAIR = 256
+PAIRS_PER_CHUNK = 3
+PAIRS = CHUNKS * PAIRS_PER_CHUNK
+HALF = 256
+
+
+def tile_plane_product_colour_features_k3_kernel(
+    tc, x_words, x_scales, u_words, u_scales, v_words, v_scales, colour, u_base, v_base, out_0, out_1, out_2
+):
+    nc = tc.nc
+    with ExitStack() as ctx:
+        keep = ctx.enter_context(tc.tile_pool(name="keep", bufs=1))
+        work = ctx.enter_context(tc.tile_pool(name="work", bufs=3))
+        psum = ctx.enter_context(tc.psum_pool(name="psum", bufs=1))
+        ctx.enter_context(tc.manual_schedule())
+
+        ident = keep.tile([P, P], F32, name="ident", align_bytes=64)
+        x_codes = keep.tile([P, PASSES, T], U32, name="x_codes", align_bytes=256)
+        x_plane = keep.tile([P, PASSES, T], U8, name="x_plane", align_bytes=256)
+        u_plane = keep.tile([P, PASSES, F], U8, name="u_plane", align_bytes=256)
+        v_plane = keep.tile([P, F], U8, name="v_plane", align_bytes=256)
+        u_codes = keep.tile([P, CHUNKS, PASSES, 2 * CHUNK], U8, name="u_codes", align_bytes=256)
+        v_codes = keep.tile([P, CHUNKS, PASSES, CHUNK], U32, name="v_codes", align_bytes=256)
+        c_rows = keep.tile([P, CHUNKS, PASSES, 4, CHUNK], BF16, name="c_rows", align_bytes=256)
+        c_quads = keep.tile([P, CHUNKS, PASSES, CHUNK * 4], BF16, name="c_quads", align_bytes=256)
+        c_codes = keep.tile([P, CHUNKS, PASSES, CHUNK], U32, name="c_codes", align_bytes=256)
+        c_plane = keep.tile([P, CHUNKS, PASSES, CHUNK], U8, name="c_plane", align_bytes=256)
+        u_cols = keep.tile([P, 16], BF16, name="u_cols", align_bytes=64)
+        v_cols = keep.tile([P, 16], BF16, name="v_cols", align_bytes=64)
+        u_cols32 = keep.tile([P, 12], F32, name="u_cols32", align_bytes=64)
+        v_cols32 = keep.tile([P, 12], F32, name="v_cols32", align_bytes=64)
+        u_bias = keep.tile([P, F], BF16, name="u_bias", align_bytes=64)
+        v_bias = keep.tile([P, F], BF16, name="v_bias", align_bytes=64)
+        y_codes = keep.tile([P, CHUNKS, T], U32, name="y_codes", align_bytes=256)
+        y_plane = keep.tile([P, CHUNKS, T], U8, name="y_plane", align_bytes=256)
+
+        def load_x(pair):
+            nc.sync.dma_start(
+                out=x_codes[:, :, pair * PAIR:(pair + 1) * PAIR].bitcast(I32),
+                in_=x_words.rearrange("g p n t -> p g (n t)")[:, :, 4 * pair * PAIR:4 * (pair + 1) * PAIR].bitcast(I32),
+            )
+
+        def load_u(c):
+            nc.sync.dma_start(
+                out=u_codes[:, c, :, :].bitcast(I32),
+                in_=u_words.rearrange("g p b -> p g b")[:, :, 2 * c * CHUNK:2 * (c + 1) * CHUNK].bitcast(I32),
+            )
+
+        def load_v(c):
+            nc.sync.dma_start(
+                out=v_codes[:, c, :, :].bitcast(I32),
+                in_=v_words.rearrange("g p n t -> p g (n t)")[:, :, 4 * c * CHUNK:4 * (c + 1) * CHUNK].bitcast(I32),
+            )
+
+        def load_c(c, g):
+            nc.sync.dma_start(
+                out=c_rows[:, c, g, :, :],
+                in_=colour[512 * g:512 * (g + 1), c * CHUNK:(c + 1) * CHUNK].rearrange("(p j) w -> p j w", j=4),
+            )
+
+        nc.vector.memset(x_plane[:].rearrange("p g n -> p (g n)").bitcast(I32), 0)
+        nc.vector.memset(u_plane[:].rearrange("p g n -> p (g n)").bitcast(I32), 0)
+        nc.vector.memset(v_plane[:].bitcast(I32), 0)
+        make_identity(nc, ident[:])
+
+        nc.sync.dma_start(
+            out=u_cols[:, 0:12].rearrange("p (c t) -> p c t", t=4),
+            in_=u_base.rearrange("(c p t) -> p c t", p=P, t=4),
+        )
+        nc.sync.dma_start(
+            out=v_cols[:, 0:12].rearrange("p (c t) -> p c t", t=4),
+            in_=v_base.rearrange("(c p t) -> p c t", p=P, t=4),
+        )
+        for q in range(4):
+            nc.sync.dma_start(
+                out=x_plane[32 * q:32 * q + 4, :, :].bitcast(I32),
+                in_=x_scales[:, 4 * q:4 * q + 4, :].rearrange("g r n -> r g n").bitcast(I32),
+            )
+        for q in range(4):
+            nc.sync.dma_start(
+                out=u_plane[32 * q:32 * q + 4, :, :].bitcast(I32),
+                in_=u_scales[:, 4 * q:4 * q + 4, :].rearrange("g r n -> r g n").bitcast(I32),
+            )
+        for q in range(4):
+            nc.gpsimd.dma_start(
+                out=v_plane[32 * q + 4:32 * q + 12, :].bitcast(I32),
+                in_=v_scales[:, 4 * q:4 * q + 4, :].bitcast(I32),
+            )
+        load_c(0, 0)
+        load_x(0)
+        load_u(0)
+        load_v(0)
+        load_c(0, 1)
+        load_x(1)
+        load_x(2)
+        for c in range(1, CHUNKS):
+            load_c(c, 0)
+            load_c(c, 1)
+            load_u(c)
+            load_v(c)
+
+        nc.vector.tensor_copy(out=u_cols32[:], in_=u_cols[:, 0:12])
+        nc.vector.tensor_copy(out=v_cols32[:], in_=v_cols[:, 0:12])
+
+        def spread_turn(cols32, c):
+            bank = psum.tile([P, 4, P], F32, name="turn_bank", tag="turn", bufs=2)
+            for t in range(4):
+                nc.tensor.transpose(bank[:, t, :], cols32[:, 4 * c + t:4 * c + t + 1].to_broadcast([P, P]), ident[:])
+            return bank
+
+        def spread_copy(bank, bias, c):
+            nc.scalar.copy(
+                out=bias[:, c * CHUNK:(c + 1) * CHUNK].rearrange("q (p t) -> q p t", t=4),
+                in_=bank[:].rearrange("q t p -> q p t"),
+            )
+
+        def interleave(engine_copy, c, g, lo, hi):
+            engine_copy(
+                out=c_quads[:, c, g, 4 * lo:4 * hi].rearrange("p (b i t) -> p b t i", i=4, t=4),
+                in_=c_rows[:, c, g, :, lo:hi].rearrange("p t (b i) -> p b t i", i=4),
+            )
+
+        def quantize_c(c, g):
+            nc.vector.quantize_mx(out=c_codes[:, c, g, :].bitcast(FP8X4), scales=c_plane[:, c, g, :], in_=c_quads[:, c, g, :])
+
+        def product(which, pair, a):
+            c = pair // PAIRS_PER_CHUNK
+            t0 = (pair % PAIRS_PER_CHUNK) * PAIR + a * P
+            cols = slice(c * CHUNK, (c + 1) * CHUNK)
+            bank = psum.tile([P, CHUNK], F32, name="bank", tag="%s%d" % (which, a))
+            for g in range(PASSES):
+                if which == "u":
+                    rhs, rhs_scale = u_codes[:, c, g, :].bitcast(FP4X4), u_plane[:, g, cols]
+                elif which == "v":
+                    rhs, rhs_scale = v_codes[:, c, g, :].bitcast(FP8X4), v_plane[4 * (g + 1):P, cols]
+                else:
+                    rhs, rhs_scale = c_codes[:, c, g, :].bitcast(FP8X4), c_plane[:, c, g, :]
+                nc.tensor.matmul_mx(
+                    out=bank[:],
+                    lhsT=x_codes[:, g, t0:t0 + P].bitcast(FP8X4),
+                    lhsT_scale=x_plane[:, g, t0:t0 + P],
+                    rhs=rhs,
+                    rhs_scale=rhs_scale,
+                    start=(g == 0),
+                    stop=(g == PASSES - 1),
+                )
+            return bank
+
+        def add_bias(dst, bank, bias, pair):
+            c = pair // PAIRS_PER_CHUNK
+            nc.vector.tensor_tensor(out=dst, in0=bank[:], in1=bias[:, c * CHUNK:(c + 1) * CHUNK], op=ADD)
+
+        planes_of = {}
+        y_of = {}
+        yb_of = {}
+        turned_of = {}
+        quads_of = {}
+
+        def finish(pair, a, bank):
+            if a == 0:
+                y_of[pair] = work.tile([P, 2, CHUNK], F32, name="y")
+            nc.vector.tensor_tensor(out=y_of[pair][:, a, :], in0=bank[:], in1=planes_of[pair][:, a, :], op=MULT)
+
+        def store_y(pair, lo, hi):
+            c = pair // PAIRS_PER_CHUNK
+            t0 = (pair % PAIRS_PER_CHUNK) * PAIR
+            nc.sync.dma_start(
+                out=out_0[t0 + lo * P:t0 + hi * P, c * CHUNK:(c + 1) * CHUNK].rearrange("(a p) f -> p a f", p=P),
+                in_=y_of[pair][:, lo:hi, :],
+            )
+
+        def round_y(pair, a):
+            if a == 0:
+                yb_of[pair] = work.tile([P, 2, CHUNK], BF16, name="y_bf", align_bytes=64)
+            nc.scalar.copy(
+                out=yb_of[pair][:, a, :].rearrange("m (u p e) -> m u p e", u=2, e=2),
+                in_=y_of[pair][:, a, :].rearrange("m (p u e) -> m u p e", u=2, e=2),
+            )
+
+        def turn_y(pair):
+            bank = psum.tile([P, 4, P], F32, name="turn_bank", tag="turn", bufs=2)
+            words = yb_of[pair][:].rearrange("m a f -> m (a f)").bitcast(F32)
+            for s in range(4):
+                nc.tensor.transpose(bank[:, s, :], words[:, s * P:(s + 1) * P], ident[:])
+            turned_of[pair] = bank
+
+        def gather_y(pair, engine_copy):
+            quads = work.tile([P, 4 * PAIR], BF16, name="y_quads", align_bytes=64)
+            engine_copy(
+                out=quads[:].bitcast(F32).rearrange("p (a m u) -> p a m u", a=2, u=2),
+                in_=turned_of[pair][:].rearrange("p (a u) m -> p a m u", a=2),
+            )
+            quads_of[pair] = quads
+
+        def quantize_y(pair):
+            c = pair // PAIRS_PER_CHUNK
+            t0 = (pair % PAIRS_PER_CHUNK) * PAIR
+            nc.vector.quantize_mx(
+                out=y_codes[:, c, t0:t0 + PAIR].bitcast(FP8X4), scales=y_plane[:, c, t0:t0 + PAIR], in_=quads_of[pair][:]
+            )
+
+        def store_codes(c, lo, hi):
+            nc.sync.dma_start(
+                out=out_1[c].rearrange("p m t -> p (m t)")[:, 4 * lo:4 * hi].bitcast(I32),
+                in_=y_codes[:, c, lo:hi].bitcast(I32),
+            )
+
+        def store_scales(lo, hi):
+            for q in range(4):
+                nc.sync.dma_start(
+                    out=out_2[lo:hi, 4 * q:4 * q + 4, :].rearrange("g r n -> r g n").bitcast(I32),
+                    in_=y_plane[32 * q:32 * q + 4, lo:hi, :].bitcast(I32),
+                )
+
+        bank_u = spread_turn(u_cols32, 0)
+        bank_v = spread_turn(v_cols32, 0)
+        spread_copy(bank_u, u_bias, 0)
+        spread_copy(bank_v, v_bias, 0)
+        interleave(nc.vector.tensor_copy, 0, 0, 0, CHUNK)
+        quantize_c(0, 0)
+
+        pieces = [(c, g, h) for c in (1, 2) for g in (0, 1) for h in (0, 1)]
+        piece_slots = {2: pieces[0:2], 3: pieces[2:4], 4: pieces[4:5], 5: pieces[5:7], 6: pieces[7:8]}
+        quantize_slots = {1: (0, 1), 3: (1, 0), 4: (1, 1), 6: (2, 0), 7: (2, 1)}
+
+        for slot in range(PAIRS + 1):
+            pair, prev, old = slot, slot - 1, slot - 2
+            last = pair == PAIRS - 1
+            mine = piece_slots.get(slot, [])
+            if old >= 0:
+                round_y(old, 0)
+                round_y(old, 1)
+            if mine:
+                c, g, h = mine[0]
+                interleave(nc.scalar.copy, c, g, h * HALF, (h + 1) * HALF)
+            if pair < PAIRS:
+                first = work.tile([P, 2, CHUNK], F32, name="first")
+                second = work.tile([P, 2, CHUNK], F32, name="second")
+                planes_of[pair] = work.tile([P, 2, CHUNK], F32, name="planes")
+                if slot == 0:
+                    ua = product("u", pair, 0)
+                    ub = product("u", pair, 1)
+                    bank_u = spread_turn(u_cols32, 1)
+                    bank_v = spread_turn(v_cols32, 1)
+                    spread_copy(bank_u, u_bias, 1)
+                    spread_copy(bank_v, v_bias, 1)
+                    interleave(nc.scalar.copy, 0, 1, 0, CHUNK)
+                    va = product("v", pair, 0)
+                    vb = product("v", pair, 1)
+                    add_bias(first[:, 0, :], ua, u_bias, pair)
+                    add_bias(first[:, 1, :], ub, u_bias, pair)
+                    add_bias(second[:, 0, :], va, v_bias, pair)
+                    nc.gpsimd.tensor_tensor(out=planes_of[pair][:, 0, :], in0=first[:, 0, :], in1=second[:, 0, :], op=MULT)
+                    add_bias(second[:, 1, :], vb, v_bias, pair)
+                else:
+                    ua = product("u", pair, 0)
+                    va = product("v", pair, 0)
+                    ub = product("u", pair, 1)
+                    vb = product("v", pair, 1)
+                    add_bias(first[:, 0, :], ua, u_bias, pair)
+                    add_bias(second[:, 0, :], va, v_bias, pair)
+                    if last:
+                        nc.gpsimd.tensor_tensor(out=planes_of[pair][:, 0, :], in0=first[:, 0, :], in1=second[:, 0, :], op=MULT)
+                    add_bias(first[:, 1, :], ub, u_bias, pair)
+                    if slot in quantize_slots:
+                        quantize_c(*quantize_slots[slot])
+                    if slot >= 3 and not last:
+                        quantize_y(slot - 3)
+                    add_bias(second[:, 1, :], vb, v_bias, pair)
+                if last or slot == 0:
+                    nc.gpsimd.tensor_tensor(out=planes_of[pair][:, 1, :], in0=first[:, 1, :], in1=second[:, 1, :], op=MULT)
+                else:
+                    nc.gpsimd.tensor_tensor(out=planes_of[pair][:], in0=first[:], in1=second[:], op=MULT)
+            if slot == 5:
+                store_codes(0, 0, T)
+                store_scales(0, 1)
+            if slot == 7:
+                store_codes(1, 0, 2 * PAIR)
+            if slot == 1:
+                bank_u = spread_turn(u_cols32, 2)
+                bank_v = spread_turn(v_cols32, 2)
+                spread_copy(bank_u, u_bias, 2)
+                spread_copy(bank_v, v_bias, 2)
+            if old >= 0 and slot < PAIRS:
+                turn_y(old)
+                gather_y(old, nc.scalar.copy)
+            if len(mine) > 1:
+                c, g, h = mine[1]
+                interleave(nc.scalar.copy, c, g, h * HALF, (h + 1) * HALF)
+            if prev >= 0:
+                ca = product("c", prev, 0)
+                cb = product("c", prev, 1)
+                finish(prev, 0, ca)
+                if prev == PAIRS - 1:
+                    store_y(prev, 0, 1)
+                finish(prev, 1, cb)
+                if prev == PAIRS - 1:
+                    store_y(prev, 1, 2)
+                else:
+                    store_y(prev, 0, 2)
+        round_y(8, 0)
+        turn_y(7)
+        round_y(8, 1)
+        quantize_y(5)
+        quantize_y(6)
+        gather_y(7, nc.vector.tensor_copy)
+        turn_y(8)
+        gather_y(8, nc.scalar.copy)
+        store_codes(1, 2 * PAIR, T)
+        quantize_y(7)
+        store_codes(2, 0, 2 * PAIR)
+        quantize_y(8)
+        store_codes(2, 2 * PAIR, T)
+        store_scales(1, 3)

@@ -37,9 +37,10 @@ def tile_plane_product_colour_features_k3_kernel(
         ctx.enter_context(tc.manual_schedule())
 
         ident = keep.tile([P, P], F32, name="ident", align_bytes=64)
-        x_codes = keep.tile([P, PASSES, T], U32, name="x_codes", align_bytes=256)
+        x_codes = keep.tile([P, PAIRS_PER_CHUNK, PASSES, PAIR], U32, name="x_codes", align_bytes=256)
         x_plane = keep.tile([P, PASSES, T], U8, name="x_plane", align_bytes=256)
-        u_plane = keep.tile([P, PASSES, F], U8, name="u_plane", align_bytes=256)
+        u_plane_head = keep.tile([P, PASSES, CHUNK], U8, name="u_plane_head", align_bytes=256)
+        u_plane_rest = keep.tile([P, PASSES, F - CHUNK], U8, name="u_plane_rest", align_bytes=256)
         v_plane = keep.tile([P, F], U8, name="v_plane", align_bytes=256)
         u_codes = keep.tile([P, CHUNKS, PASSES, 2 * CHUNK], U8, name="u_codes", align_bytes=256)
         v_codes = keep.tile([P, CHUNKS, PASSES, CHUNK], U32, name="v_codes", align_bytes=256)
@@ -58,7 +59,7 @@ def tile_plane_product_colour_features_k3_kernel(
 
         def load_x(pair):
             nc.sync.dma_start(
-                out=x_codes[:, :, pair * PAIR:(pair + 1) * PAIR].bitcast(I32),
+                out=x_codes[:, pair, :, :].bitcast(I32),
                 in_=x_words.rearrange("g p n t -> p g (n t)")[:, :, 4 * pair * PAIR:4 * (pair + 1) * PAIR].bitcast(I32),
             )
 
@@ -80,46 +81,56 @@ def tile_plane_product_colour_features_k3_kernel(
                 in_=colour[512 * g:512 * (g + 1), c * CHUNK:(c + 1) * CHUNK].rearrange("(p j) w -> p j w", j=4),
             )
 
-        nc.vector.memset(x_plane[:].rearrange("p g n -> p (g n)").bitcast(I32), 0)
-        nc.vector.memset(u_plane[:].rearrange("p g n -> p (g n)").bitcast(I32), 0)
-        nc.vector.memset(v_plane[:].bitcast(I32), 0)
-        make_identity(nc, ident[:])
+        def load_cols(queue, cols, base):
+            queue.dma_start(
+                out=cols[:, 0:12].rearrange("p (c t) -> p c t", t=4),
+                in_=base.rearrange("(c p t) -> p c t", p=P, t=4),
+            )
 
-        nc.sync.dma_start(
-            out=u_cols[:, 0:12].rearrange("p (c t) -> p c t", t=4),
-            in_=u_base.rearrange("(c p t) -> p c t", p=P, t=4),
-        )
-        nc.sync.dma_start(
-            out=v_cols[:, 0:12].rearrange("p (c t) -> p c t", t=4),
-            in_=v_base.rearrange("(c p t) -> p c t", p=P, t=4),
-        )
-        for q in range(4):
+        def load_plane(plane, scales, r, lo, hi):
             nc.sync.dma_start(
-                out=x_plane[32 * q:32 * q + 4, :, :].bitcast(I32),
-                in_=x_scales[:, 4 * q:4 * q + 4, :].rearrange("g r n -> r g n").bitcast(I32),
+                out=plane[r:P:32, :, :].bitcast(I32),
+                in_=scales[:, r:16:4, lo:hi].rearrange("g q n -> q g n").bitcast(I32),
             )
-        for q in range(4):
+
+        def load_v_plane(q, lo, hi):
             nc.sync.dma_start(
-                out=u_plane[32 * q:32 * q + 4, :, :].bitcast(I32),
-                in_=u_scales[:, 4 * q:4 * q + 4, :].rearrange("g r n -> r g n").bitcast(I32),
+                out=v_plane[32 * q + 4:32 * q + 12, lo:hi].bitcast(I32),
+                in_=v_scales[:, 4 * q:4 * q + 4, lo:hi].bitcast(I32),
             )
-        for q in range(4):
-            nc.gpsimd.dma_start(
-                out=v_plane[32 * q + 4:32 * q + 12, :].bitcast(I32),
-                in_=v_scales[:, 4 * q:4 * q + 4, :].bitcast(I32),
-            )
+
+        nc.vector.memset(x_plane[:].rearrange("p g n -> p (g n)").bitcast(I32), 0)
+        nc.vector.memset(u_plane_head[:].rearrange("p g n -> p (g n)").bitcast(I32), 0)
+        nc.vector.memset(v_plane[:].bitcast(I32), 0)
+        nc.vector.memset(u_plane_rest[:].rearrange("p g n -> p (g n)").bitcast(I32), 0)
+        make_identity(nc, ident[:])
+        load_cols(nc.sync, u_cols, u_base)
+        load_cols(nc.sync, v_cols, v_base)
+        for r in range(4):
+            load_plane(x_plane, x_scales, r, 0, T)
         load_c(0, 0)
         load_x(0)
+        for r in range(4):
+            load_plane(u_plane_head, u_scales, r, 0, CHUNK)
         load_u(0)
         load_v(0)
-        load_c(0, 1)
+        for q in range(4):
+            load_v_plane(q, 0, CHUNK)
         load_x(1)
+        load_c(0, 1)
         load_x(2)
-        for c in range(1, CHUNKS):
-            load_c(c, 0)
-            load_c(c, 1)
-            load_u(c)
-            load_v(c)
+        for r in range(4):
+            load_plane(u_plane_rest, u_scales, r, CHUNK, F)
+        for q in range(4):
+            load_v_plane(q, CHUNK, F)
+        load_u(1)
+        load_v(1)
+        load_c(1, 0)
+        load_c(1, 1)
+        load_u(2)
+        load_v(2)
+        load_c(2, 0)
+        load_c(2, 1)
 
         nc.vector.tensor_copy(out=u_cols32[:], in_=u_cols[:, 0:12])
         nc.vector.tensor_copy(out=v_cols32[:], in_=v_cols[:, 0:12])
@@ -145,21 +156,22 @@ def tile_plane_product_colour_features_k3_kernel(
         def quantize_c(c, g):
             nc.vector.quantize_mx(out=c_codes[:, c, g, :].bitcast(FP8X4), scales=c_plane[:, c, g, :], in_=c_quads[:, c, g, :])
 
-        def product(which, pair, a):
+        def product(which, pair, a, tag=None):
             c = pair // PAIRS_PER_CHUNK
             t0 = (pair % PAIRS_PER_CHUNK) * PAIR + a * P
             cols = slice(c * CHUNK, (c + 1) * CHUNK)
-            bank = psum.tile([P, CHUNK], F32, name="bank", tag="%s%d" % (which, a))
+            bank = psum.tile([P, CHUNK], F32, name="bank", tag=tag or "%s%d" % (which, a))
             for g in range(PASSES):
                 if which == "u":
-                    rhs, rhs_scale = u_codes[:, c, g, :].bitcast(FP4X4), u_plane[:, g, cols]
+                    rhs = u_codes[:, c, g, :].bitcast(FP4X4)
+                    rhs_scale = u_plane_head[:, g, :] if c == 0 else u_plane_rest[:, g, (c - 1) * CHUNK:c * CHUNK]
                 elif which == "v":
                     rhs, rhs_scale = v_codes[:, c, g, :].bitcast(FP8X4), v_plane[4 * (g + 1):P, cols]
                 else:
                     rhs, rhs_scale = c_codes[:, c, g, :].bitcast(FP8X4), c_plane[:, c, g, :]
                 nc.tensor.matmul_mx(
                     out=bank[:],
-                    lhsT=x_codes[:, g, t0:t0 + P].bitcast(FP8X4),
+                    lhsT=x_codes[:, pair % PAIRS_PER_CHUNK, g, a * P:(a + 1) * P].bitcast(FP8X4),
                     lhsT_scale=x_plane[:, g, t0:t0 + P],
                     rhs=rhs,
                     rhs_scale=rhs_scale,
@@ -178,10 +190,18 @@ def tile_plane_product_colour_features_k3_kernel(
         turned_of = {}
         quads_of = {}
 
+        def y_tile(pair):
+            if pair not in y_of:
+                y_of[pair] = work.tile([P, 2, CHUNK], F32, name="y", bufs=4)
+            return y_of[pair]
+
         def finish(pair, a, bank):
-            if a == 0:
-                y_of[pair] = work.tile([P, 2, CHUNK], F32, name="y")
-            nc.vector.tensor_tensor(out=y_of[pair][:, a, :], in0=bank[:], in1=planes_of[pair][:, a, :], op=MULT)
+            nc.vector.tensor_tensor(out=y_tile(pair)[:, a, :], in0=bank[:], in1=planes_of[pair][:, a, :], op=MULT)
+
+        def finish_aside(pair, a, bank):
+            basis = work.tile([P, CHUNK], F32, name="basis")
+            nc.scalar.copy(out=basis[:], in_=bank[:])
+            nc.gpsimd.tensor_tensor(out=y_tile(pair)[:, a, :], in0=basis[:], in1=planes_of[pair][:, a, :], op=MULT)
 
         def store_y(pair, lo, hi):
             c = pair // PAIRS_PER_CHUNK
@@ -191,34 +211,37 @@ def tile_plane_product_colour_features_k3_kernel(
                 in_=y_of[pair][:, lo:hi, :],
             )
 
-        def round_y(pair, a):
-            if a == 0:
+        def round_y(pair, lo, hi):
+            if pair not in yb_of:
                 yb_of[pair] = work.tile([P, 2, CHUNK], BF16, name="y_bf", align_bytes=64)
-            nc.scalar.copy(
-                out=yb_of[pair][:, a, :].rearrange("m (u p e) -> m u p e", u=2, e=2),
-                in_=y_of[pair][:, a, :].rearrange("m (p u e) -> m u p e", u=2, e=2),
-            )
+            for a in range(lo, hi):
+                nc.scalar.copy(
+                    out=yb_of[pair][:, a, :].rearrange("m (u p e) -> m u p e", u=2, e=2),
+                    in_=y_of[pair][:, a, :].rearrange("m (p u e) -> m u p e", u=2, e=2),
+                )
 
-        def turn_y(pair):
-            bank = psum.tile([P, 4, P], F32, name="turn_bank", tag="turn", bufs=2)
+        def turn_y(pair, lo, hi, tag="turn", bufs=2):
+            bank = psum.tile([P, 4, P], F32, name="turn_bank", tag=tag, bufs=bufs)
             words = yb_of[pair][:].rearrange("m a f -> m (a f)").bitcast(F32)
-            for s in range(4):
+            for s in range(2 * lo, 2 * hi):
                 nc.tensor.transpose(bank[:, s, :], words[:, s * P:(s + 1) * P], ident[:])
-            turned_of[pair] = bank
+            turned_of[pair, lo] = bank
 
-        def gather_y(pair, engine_copy):
-            quads = work.tile([P, 4 * PAIR], BF16, name="y_quads", align_bytes=64)
+        def gather_y(pair, lo, hi, engine_copy):
+            if pair // 2 not in quads_of:
+                quads_of[pair // 2] = work.tile([P, 2, 4 * PAIR], BF16, name="y_quads", align_bytes=64)
             engine_copy(
-                out=quads[:].bitcast(F32).rearrange("p (a m u) -> p a m u", a=2, u=2),
-                in_=turned_of[pair][:].rearrange("p (a u) m -> p a m u", a=2),
+                out=quads_of[pair // 2][:, pair % 2, :].bitcast(F32).rearrange("p (a m u) -> p a m u", a=2, u=2)[:, lo:hi],
+                in_=turned_of[pair, lo][:].rearrange("p (a u) m -> p a m u", a=2)[:, lo:hi],
             )
-            quads_of[pair] = quads
 
-        def quantize_y(pair):
-            c = pair // PAIRS_PER_CHUNK
-            t0 = (pair % PAIRS_PER_CHUNK) * PAIR
+        def quantize_y(tile0, tiles):
+            lo, hi = tile0 * P, (tile0 + tiles) * P
+            within = (tile0 % 4) * 4 * P
             nc.vector.quantize_mx(
-                out=y_codes[:, c, t0:t0 + PAIR].bitcast(FP8X4), scales=y_plane[:, c, t0:t0 + PAIR], in_=quads_of[pair][:]
+                out=y_codes[:].rearrange("p c t -> p (c t)")[:, lo:hi].bitcast(FP8X4),
+                scales=y_plane[:].rearrange("p c t -> p (c t)")[:, lo:hi],
+                in_=quads_of[tile0 // 4][:].rearrange("p s w -> p (s w)")[:, within:within + tiles * 4 * P],
             )
 
         def store_codes(c, lo, hi):
@@ -227,110 +250,155 @@ def tile_plane_product_colour_features_k3_kernel(
                 in_=y_codes[:, c, lo:hi].bitcast(I32),
             )
 
-        def store_scales(lo, hi):
+        def store_scales(lo, hi, queues):
             for q in range(4):
-                nc.sync.dma_start(
+                queues[q % len(queues)].dma_start(
                     out=out_2[lo:hi, 4 * q:4 * q + 4, :].rearrange("g r n -> r g n").bitcast(I32),
                     in_=y_plane[32 * q:32 * q + 4, lo:hi, :].bitcast(I32),
                 )
 
-        bank_u = spread_turn(u_cols32, 0)
-        bank_v = spread_turn(v_cols32, 0)
-        spread_copy(bank_u, u_bias, 0)
-        spread_copy(bank_v, v_bias, 0)
+        def spread(c):
+            bank_u = spread_turn(u_cols32, c)
+            bank_v = spread_turn(v_cols32, c)
+            spread_copy(bank_u, u_bias, c)
+            spread_copy(bank_v, v_bias, c)
+
+        def piece(c, g, h):
+            interleave(nc.scalar.copy, c, g, h * HALF, (h + 1) * HALF)
+
+        def multiply_planes(pair, lo, hi, first, second):
+            nc.gpsimd.tensor_tensor(
+                out=planes_of[pair][:, lo:hi, :], in0=first[:, lo:hi, :], in1=second[:, lo:hi, :], op=MULT
+            )
+
+        state = {}
+
+        def planes_step(pair, quantize_now):
+            first = work.tile([P, 2, CHUNK], F32, name="first")
+            second = work.tile([P, 2, CHUNK], F32, name="second")
+            planes_of[pair] = work.tile([P, 2, CHUNK], F32, name="planes", bufs=4)
+            if pair == 0:
+                ua = product("u", pair, 0)
+                ub = product("u", pair, 1)
+                va = product("v", pair, 0)
+                vb = product("v", pair, 1)
+                add_bias(first[:, 0, :], ua, u_bias, pair)
+                add_bias(first[:, 1, :], ub, u_bias, pair)
+                add_bias(second[:, 0, :], va, v_bias, pair)
+                multiply_planes(pair, 0, 1, first, second)
+            else:
+                ua = product("u", pair, 0)
+                va = product("v", pair, 0)
+                ub = product("u", pair, 1)
+                vb = product("v", pair, 1)
+                add_bias(first[:, 0, :], ua, u_bias, pair)
+                add_bias(second[:, 0, :], va, v_bias, pair)
+                if pair == PAIRS - 1:
+                    multiply_planes(pair, 0, 1, first, second)
+                add_bias(first[:, 1, :], ub, u_bias, pair)
+            for step in quantize_now:
+                step[0](*step[1:])
+            add_bias(second[:, 1, :], vb, v_bias, pair)
+            multiply_planes(pair, 1 if pair in (0, PAIRS - 1) else 0, 2, first, second)
+
+        def basis_step(pair, a):
+            finish(pair, a, product("c", pair, a, ("u0", "v0")[a] if pair == PAIRS - 1 else None))
+
+        def aside_step(pair, a):
+            finish_aside(pair, a, product("c", pair, a))
+
+        def turn_step(pair):
+            turn_y(pair, 0, 2)
+            gather_y(pair, 0, 2, nc.scalar.copy)
+
+        def spread_one(cols32, bias, c):
+            spread_copy(spread_turn(cols32, c), bias, c)
+
+        spread_one(u_cols32, u_bias, 0)
+        spread_one(v_cols32, v_bias, 0)
         interleave(nc.vector.tensor_copy, 0, 0, 0, CHUNK)
         quantize_c(0, 0)
-
-        pieces = [(c, g, h) for c in (1, 2) for g in (0, 1) for h in (0, 1)]
-        piece_slots = {2: pieces[0:2], 3: pieces[2:4], 4: pieces[4:5], 5: pieces[5:7], 6: pieces[7:8]}
-        quantize_slots = {1: (0, 1), 3: (1, 0), 4: (1, 1), 6: (2, 0), 7: (2, 1)}
-
-        for slot in range(PAIRS + 1):
-            pair, prev, old = slot, slot - 1, slot - 2
-            last = pair == PAIRS - 1
-            mine = piece_slots.get(slot, [])
-            if old >= 0:
-                round_y(old, 0)
-                round_y(old, 1)
-            if mine:
-                c, g, h = mine[0]
-                interleave(nc.scalar.copy, c, g, h * HALF, (h + 1) * HALF)
-            if pair < PAIRS:
-                first = work.tile([P, 2, CHUNK], F32, name="first")
-                second = work.tile([P, 2, CHUNK], F32, name="second")
-                planes_of[pair] = work.tile([P, 2, CHUNK], F32, name="planes")
-                if slot == 0:
-                    ua = product("u", pair, 0)
-                    ub = product("u", pair, 1)
-                    bank_u = spread_turn(u_cols32, 1)
-                    bank_v = spread_turn(v_cols32, 1)
-                    spread_copy(bank_u, u_bias, 1)
-                    spread_copy(bank_v, v_bias, 1)
-                    interleave(nc.scalar.copy, 0, 1, 0, CHUNK)
-                    va = product("v", pair, 0)
-                    vb = product("v", pair, 1)
-                    add_bias(first[:, 0, :], ua, u_bias, pair)
-                    add_bias(first[:, 1, :], ub, u_bias, pair)
-                    add_bias(second[:, 0, :], va, v_bias, pair)
-                    nc.gpsimd.tensor_tensor(out=planes_of[pair][:, 0, :], in0=first[:, 0, :], in1=second[:, 0, :], op=MULT)
-                    add_bias(second[:, 1, :], vb, v_bias, pair)
-                else:
-                    ua = product("u", pair, 0)
-                    va = product("v", pair, 0)
-                    ub = product("u", pair, 1)
-                    vb = product("v", pair, 1)
-                    add_bias(first[:, 0, :], ua, u_bias, pair)
-                    add_bias(second[:, 0, :], va, v_bias, pair)
-                    if last:
-                        nc.gpsimd.tensor_tensor(out=planes_of[pair][:, 0, :], in0=first[:, 0, :], in1=second[:, 0, :], op=MULT)
-                    add_bias(first[:, 1, :], ub, u_bias, pair)
-                    if slot in quantize_slots:
-                        quantize_c(*quantize_slots[slot])
-                    if slot >= 3 and not last:
-                        quantize_y(slot - 3)
-                    add_bias(second[:, 1, :], vb, v_bias, pair)
-                if last or slot == 0:
-                    nc.gpsimd.tensor_tensor(out=planes_of[pair][:, 1, :], in0=first[:, 1, :], in1=second[:, 1, :], op=MULT)
-                else:
-                    nc.gpsimd.tensor_tensor(out=planes_of[pair][:], in0=first[:], in1=second[:], op=MULT)
-            if slot == 5:
-                store_codes(0, 0, T)
-                store_scales(0, 1)
-            if slot == 7:
-                store_codes(1, 0, 2 * PAIR)
-            if slot == 1:
-                bank_u = spread_turn(u_cols32, 2)
-                bank_v = spread_turn(v_cols32, 2)
-                spread_copy(bank_u, u_bias, 2)
-                spread_copy(bank_v, v_bias, 2)
-            if old >= 0 and slot < PAIRS:
-                turn_y(old)
-                gather_y(old, nc.scalar.copy)
-            if len(mine) > 1:
-                c, g, h = mine[1]
-                interleave(nc.scalar.copy, c, g, h * HALF, (h + 1) * HALF)
-            if prev >= 0:
-                ca = product("c", prev, 0)
-                cb = product("c", prev, 1)
-                finish(prev, 0, ca)
-                if prev == PAIRS - 1:
-                    store_y(prev, 0, 1)
-                finish(prev, 1, cb)
-                if prev == PAIRS - 1:
-                    store_y(prev, 1, 2)
-                else:
-                    store_y(prev, 0, 2)
-        round_y(8, 0)
-        turn_y(7)
-        round_y(8, 1)
-        quantize_y(5)
-        quantize_y(6)
-        gather_y(7, nc.vector.tensor_copy)
-        turn_y(8)
-        gather_y(8, nc.scalar.copy)
+        planes_step(0, [])
+        piece(0, 1, 0)
+        piece(0, 1, 1)
+        planes_step(1, [(quantize_c, 0, 1)])
+        spread_one(u_cols32, u_bias, 1)
+        spread_one(v_cols32, v_bias, 1)
+        basis_step(0, 0)
+        basis_step(0, 1)
+        store_y(0, 0, 2)
+        round_y(0, 0, 2)
+        piece(1, 0, 0)
+        planes_step(2, [])
+        turn_step(0)
+        piece(1, 0, 1)
+        basis_step(1, 0)
+        basis_step(1, 1)
+        store_y(1, 0, 2)
+        round_y(1, 0, 2)
+        piece(1, 1, 0)
+        planes_step(3, [(quantize_c, 1, 0)])
+        turn_step(1)
+        piece(1, 1, 1)
+        basis_step(2, 0)
+        basis_step(2, 1)
+        store_y(2, 0, 2)
+        round_y(2, 0, 2)
+        piece(2, 0, 0)
+        planes_step(4, [(quantize_c, 1, 1), (quantize_y, 0, 4)])
+        turn_step(2)
+        spread_one(u_cols32, u_bias, 2)
+        basis_step(3, 0)
+        basis_step(3, 1)
+        store_y(3, 0, 2)
+        round_y(3, 0, 2)
+        piece(2, 0, 1)
+        planes_step(5, [(quantize_y, 4, 2)])
+        turn_step(3)
+        spread_one(v_cols32, v_bias, 2)
+        piece(2, 1, 0)
+        store_codes(0, 0, T)
+        store_scales(0, 1, [nc.sync])
+        basis_step(4, 0)
+        basis_step(4, 1)
+        store_y(4, 0, 2)
+        round_y(4, 0, 2)
+        piece(2, 1, 1)
+        planes_step(6, [(quantize_c, 2, 0), (quantize_y, 6, 2)])
+        turn_step(4)
+        basis_step(5, 0)
+        basis_step(5, 1)
+        store_y(5, 0, 2)
+        round_y(5, 0, 2)
+        planes_step(7, [(quantize_c, 2, 1), (quantize_y, 8, 2)])
+        turn_step(5)
+        store_codes(1, 0, 2 * PAIR)
+        basis_step(6, 0)
+        basis_step(6, 1)
+        store_y(6, 0, 2)
+        round_y(6, 0, 2)
+        planes_step(8, [])
+        turn_step(6)
+        basis_step(7, 0)
+        basis_step(7, 1)
+        store_y(7, 0, 2)
+        round_y(7, 0, 2)
+        basis_step(8, 0)
+        store_y(8, 0, 1)
+        basis_step(8, 1)
+        store_y(8, 1, 2)
+        round_y(8, 0, 1)
+        turn_y(7, 0, 2)
+        gather_y(7, 0, 2, nc.vector.tensor_copy)
+        turn_y(8, 0, 1)
+        round_y(8, 1, 2)
+        gather_y(8, 0, 1, nc.scalar.copy)
+        turn_y(8, 1, 2, "c0", 1)
+        gather_y(8, 1, 2, nc.scalar.copy)
+        quantize_y(10, 2)
         store_codes(1, 2 * PAIR, T)
-        quantize_y(7)
+        quantize_y(12, 4)
         store_codes(2, 0, 2 * PAIR)
-        quantize_y(8)
+        quantize_y(16, 2)
         store_codes(2, 2 * PAIR, T)
-        store_scales(1, 3)
+        store_scales(1, 3, [nc.sync, nc.scalar])

@@ -119,24 +119,24 @@ def tile_plane_product_colour_features_k3_kernel(
         load_x(1)
         load_c(0, 1)
         load_x(2)
+        load_c(1, 0)
         for r in range(4):
             load_plane(u_plane_rest, u_scales, r, CHUNK, F)
         for q in range(4):
             load_v_plane(q, CHUNK, F)
+        load_c(1, 1)
         load_u(1)
         load_v(1)
-        load_c(1, 0)
-        load_c(1, 1)
-        load_u(2)
-        load_v(2)
         load_c(2, 0)
         load_c(2, 1)
+        load_u(2)
+        load_v(2)
 
         nc.vector.tensor_copy(out=u_cols32[:], in_=u_cols[:, 0:12])
         nc.vector.tensor_copy(out=v_cols32[:], in_=v_cols[:, 0:12])
 
-        def spread_turn(cols32, c):
-            bank = psum.tile([P, 4, P], F32, name="turn_bank", tag="turn", bufs=2)
+        def spread_turn(cols32, c, tag="turn", bufs=2):
+            bank = psum.tile([P, 4, P], F32, name="turn_bank", tag=tag, bufs=bufs)
             for t in range(4):
                 nc.tensor.transpose(bank[:, t, :], cols32[:, 4 * c + t:4 * c + t + 1].to_broadcast([P, P]), ident[:])
             return bank
@@ -298,11 +298,20 @@ def tile_plane_product_colour_features_k3_kernel(
                 add_bias(first[:, 1, :], ub, u_bias, pair)
             for step in quantize_now:
                 step[0](*step[1:])
-            add_bias(second[:, 1, :], vb, v_bias, pair)
+            if pair == 0:
+                add_bias(second[:, 1, :], vb, v_bias, pair)
+            else:
+                add_bias(second[:, 1, :], vb, v_bias, pair)
             multiply_planes(pair, 1 if pair in (0, PAIRS - 1) else 0, 2, first, second)
 
         def basis_step(pair, a):
             finish(pair, a, product("c", pair, a, ("u0", "v0")[a] if pair == PAIRS - 1 else None))
+
+        def basis_pair(pair):
+            ca = product("c", pair, 0)
+            cb = product("c", pair, 1)
+            finish(pair, 1, cb)
+            finish(pair, 0, ca)
 
         def aside_step(pair, a):
             finish_aside(pair, a, product("c", pair, a))
@@ -311,71 +320,71 @@ def tile_plane_product_colour_features_k3_kernel(
             turn_y(pair, 0, 2)
             gather_y(pair, 0, 2, nc.scalar.copy)
 
-        def spread_one(cols32, bias, c):
-            spread_copy(spread_turn(cols32, c), bias, c)
+        def spread_one(cols32, bias, c, tag="turn", bufs=2):
+            spread_copy(spread_turn(cols32, c, tag, bufs), bias, c)
 
         spread_one(u_cols32, u_bias, 0)
         spread_one(v_cols32, v_bias, 0)
+        spread_one(u_cols32, u_bias, 1, "c0", 1)
+        spread_one(v_cols32, v_bias, 1, "c1", 1)
         interleave(nc.vector.tensor_copy, 0, 0, 0, CHUNK)
         quantize_c(0, 0)
         planes_step(0, [])
         piece(0, 1, 0)
         piece(0, 1, 1)
         planes_step(1, [(quantize_c, 0, 1)])
-        spread_one(u_cols32, u_bias, 1)
-        spread_one(v_cols32, v_bias, 1)
+        spread_one(u_cols32, u_bias, 2)
+        spread_one(v_cols32, v_bias, 2)
+        piece(1, 0, 0)
         basis_step(0, 0)
         basis_step(0, 1)
         store_y(0, 0, 2)
-        round_y(0, 0, 2)
-        piece(1, 0, 0)
-        planes_step(2, [])
-        turn_step(0)
         piece(1, 0, 1)
+        round_y(0, 0, 2)
+        piece(1, 1, 0)
+        planes_step(2, [(quantize_c, 1, 0)])
         basis_step(1, 0)
         basis_step(1, 1)
         store_y(1, 0, 2)
-        round_y(1, 0, 2)
-        piece(1, 1, 0)
-        planes_step(3, [(quantize_c, 1, 0)])
-        turn_step(1)
         piece(1, 1, 1)
+        round_y(1, 0, 2)
+        planes_step(3, [(quantize_c, 1, 1)])
         basis_step(2, 0)
         basis_step(2, 1)
         store_y(2, 0, 2)
-        round_y(2, 0, 2)
         piece(2, 0, 0)
-        planes_step(4, [(quantize_c, 1, 1), (quantize_y, 0, 4)])
-        turn_step(2)
-        spread_one(u_cols32, u_bias, 2)
+        turn_step(0)
+        turn_step(1)
+        round_y(2, 0, 2)
+        piece(2, 0, 1)
+        planes_step(4, [(quantize_y, 0, 4)])
         basis_step(3, 0)
         basis_step(3, 1)
         store_y(3, 0, 2)
-        round_y(3, 0, 2)
-        piece(2, 0, 1)
-        planes_step(5, [(quantize_y, 4, 2)])
-        turn_step(3)
-        spread_one(v_cols32, v_bias, 2)
         piece(2, 1, 0)
-        store_codes(0, 0, T)
-        store_scales(0, 1, [nc.sync])
+        round_y(3, 0, 2)
+        piece(2, 1, 1)
+        planes_step(5, [(quantize_c, 2, 0)])
         basis_step(4, 0)
         basis_step(4, 1)
         store_y(4, 0, 2)
+        turn_step(2)
+        turn_step(3)
         round_y(4, 0, 2)
-        piece(2, 1, 1)
-        planes_step(6, [(quantize_c, 2, 0), (quantize_y, 6, 2)])
-        turn_step(4)
+        planes_step(6, [(quantize_c, 2, 1), (quantize_y, 4, 4)])
+        store_codes(0, 0, T)
+        store_scales(0, 1, [nc.sync])
+        store_codes(1, 0, PAIR)
         basis_step(5, 0)
         basis_step(5, 1)
         store_y(5, 0, 2)
         round_y(5, 0, 2)
-        planes_step(7, [(quantize_c, 2, 1), (quantize_y, 8, 2)])
-        turn_step(5)
-        store_codes(1, 0, 2 * PAIR)
+        planes_step(7, [])
         basis_step(6, 0)
         basis_step(6, 1)
         store_y(6, 0, 2)
+        turn_step(4)
+        turn_step(5)
         round_y(6, 0, 2)
         planes_step(8, [])
         turn_step(6)
@@ -395,10 +404,10 @@ def tile_plane_product_colour_features_k3_kernel(
         gather_y(8, 0, 1, nc.scalar.copy)
         turn_y(8, 1, 2, "c0", 1)
         gather_y(8, 1, 2, nc.scalar.copy)
-        quantize_y(10, 2)
-        store_codes(1, 2 * PAIR, T)
+        quantize_y(8, 4)
+        store_codes(1, PAIR, T)
         quantize_y(12, 4)
         store_codes(2, 0, 2 * PAIR)
         quantize_y(16, 2)
         store_codes(2, 2 * PAIR, T)
-        store_scales(1, 3, [nc.sync, nc.scalar])
+        store_scales(1, 3, [nc.scalar])

@@ -50,8 +50,7 @@ def tile_plane_product_colour_features_k3_kernel(
         c_plane = keep.tile([P, CHUNKS, PASSES, CHUNK], U8, name="c_plane", align_bytes=256)
         u_cols = keep.tile([P, 16], BF16, name="u_cols", align_bytes=64)
         v_cols = keep.tile([P, 16], BF16, name="v_cols", align_bytes=64)
-        u_cols32 = keep.tile([P, 12], F32, name="u_cols32", align_bytes=64)
-        v_cols32 = keep.tile([P, 12], F32, name="v_cols32", align_bytes=64)
+        ident_bf = keep.tile([P, P], BF16, name="ident_bf", align_bytes=64)
         u_bias = keep.tile([P, F], BF16, name="u_bias", align_bytes=64)
         v_bias = keep.tile([P, F], BF16, name="v_bias", align_bytes=64)
         y_codes = keep.tile([P, CHUNKS, T], U32, name="y_codes", align_bytes=256)
@@ -103,6 +102,7 @@ def tile_plane_product_colour_features_k3_kernel(
         nc.vector.memset(u_plane_head[:].rearrange("p g n -> p (g n)").bitcast(I32), 0)
         nc.vector.memset(v_plane[:].bitcast(I32), 0)
         nc.vector.memset(u_plane_rest[:].rearrange("p g n -> p (g n)").bitcast(I32), 0)
+        make_identity(nc, ident_bf[:])
         make_identity(nc, ident[:])
         load_cols(nc.sync, u_cols, u_base)
         load_cols(nc.sync, v_cols, v_base)
@@ -132,13 +132,11 @@ def tile_plane_product_colour_features_k3_kernel(
         load_u(2)
         load_v(2)
 
-        nc.vector.tensor_copy(out=u_cols32[:], in_=u_cols[:, 0:12])
-        nc.vector.tensor_copy(out=v_cols32[:], in_=v_cols[:, 0:12])
 
-        def spread_turn(cols32, c, tag="turn", bufs=2):
-            bank = psum.tile([P, 4, P], F32, name="turn_bank", tag=tag, bufs=bufs)
+        def spread_turn(cols, c, tag="turn", bufs=2):
+            bank = psum.tile([P, 4, P], BF16, name="turn_bank", tag=tag, bufs=bufs)
             for t in range(4):
-                nc.tensor.transpose(bank[:, t, :], cols32[:, 4 * c + t:4 * c + t + 1].to_broadcast([P, P]), ident[:])
+                nc.tensor.transpose(bank[:, t, :], cols[:, 4 * c + t:4 * c + t + 1].to_broadcast([P, P]), ident_bf[:])
             return bank
 
         def spread_copy(bank, bias, c):
@@ -184,11 +182,12 @@ def tile_plane_product_colour_features_k3_kernel(
             c = pair // PAIRS_PER_CHUNK
             nc.vector.tensor_tensor(out=dst, in0=bank[:], in1=bias[:, c * CHUNK:(c + 1) * CHUNK], op=ADD)
 
+        yb_last = keep.tile([P, CHUNK], BF16, name="yb_last", align_bytes=64)
         planes_of = {}
         y_of = {}
         yb_of = {}
         turned_of = {}
-        quads_of = {}
+        y_quads = keep.tile([P, PAIRS, 4 * PAIR], BF16, name="y_quads", align_bytes=64)
 
         def y_tile(pair):
             if pair not in y_of:
@@ -228,20 +227,17 @@ def tile_plane_product_colour_features_k3_kernel(
             turned_of[pair, lo] = bank
 
         def gather_y(pair, lo, hi, engine_copy):
-            if pair // 2 not in quads_of:
-                quads_of[pair // 2] = work.tile([P, 2, 4 * PAIR], BF16, name="y_quads", align_bytes=64)
             engine_copy(
-                out=quads_of[pair // 2][:, pair % 2, :].bitcast(F32).rearrange("p (a m u) -> p a m u", a=2, u=2)[:, lo:hi],
+                out=y_quads[:, pair, :].bitcast(F32).rearrange("p (a m u) -> p a m u", a=2, u=2)[:, lo:hi],
                 in_=turned_of[pair, lo][:].rearrange("p (a u) m -> p a m u", a=2)[:, lo:hi],
             )
 
         def quantize_y(tile0, tiles):
             lo, hi = tile0 * P, (tile0 + tiles) * P
-            within = (tile0 % 4) * 4 * P
             nc.vector.quantize_mx(
                 out=y_codes[:].rearrange("p c t -> p (c t)")[:, lo:hi].bitcast(FP8X4),
                 scales=y_plane[:].rearrange("p c t -> p (c t)")[:, lo:hi],
-                in_=quads_of[tile0 // 4][:].rearrange("p s w -> p (s w)")[:, within:within + tiles * 4 * P],
+                in_=y_quads[:].rearrange("p s w -> p (s w)")[:, 4 * lo:4 * hi],
             )
 
         def store_codes(c, lo, hi):
@@ -258,8 +254,8 @@ def tile_plane_product_colour_features_k3_kernel(
                 )
 
         def spread(c):
-            bank_u = spread_turn(u_cols32, c)
-            bank_v = spread_turn(v_cols32, c)
+            bank_u = spread_turn(u_cols, c)
+            bank_v = spread_turn(v_cols, c)
             spread_copy(bank_u, u_bias, c)
             spread_copy(bank_v, v_bias, c)
 
@@ -273,7 +269,7 @@ def tile_plane_product_colour_features_k3_kernel(
 
         state = {}
 
-        def planes_step(pair, quantize_now):
+        def planes_step(pair, quantize_now, between=()):
             first = work.tile([P, 2, CHUNK], F32, name="first")
             second = work.tile([P, 2, CHUNK], F32, name="second")
             planes_of[pair] = work.tile([P, 2, CHUNK], F32, name="planes", bufs=4)
@@ -289,12 +285,18 @@ def tile_plane_product_colour_features_k3_kernel(
             else:
                 ua = product("u", pair, 0)
                 va = product("v", pair, 0)
-                ub = product("u", pair, 1)
-                vb = product("v", pair, 1)
                 add_bias(first[:, 0, :], ua, u_bias, pair)
+                if pair == PAIRS - 1:
+                    for step in quantize_now:
+                        step[0](*step[1:])
+                    quantize_now = []
                 add_bias(second[:, 0, :], va, v_bias, pair)
                 if pair == PAIRS - 1:
                     multiply_planes(pair, 0, 1, first, second)
+                for step in between:
+                    step[0](*step[1:])
+                ub = product("u", pair, 1)
+                vb = product("v", pair, 1)
                 add_bias(first[:, 1, :], ub, u_bias, pair)
             for step in quantize_now:
                 step[0](*step[1:])
@@ -313,6 +315,18 @@ def tile_plane_product_colour_features_k3_kernel(
             finish(pair, 1, cb)
             finish(pair, 0, ca)
 
+        def last_tile():
+            bank = product("c", 8, 1, "v0")
+            nc.vector.tensor_tensor(out=yb_last[:], in0=bank[:], in1=planes_of[8][:, 1, :], op=MULT)
+            finish(8, 1, bank)
+
+        def turn_last():
+            bank = psum.tile([P, 4, P], F32, name="turn_bank", tag="c0", bufs=1)
+            words = yb_last[:].bitcast(F32)
+            for u in range(2):
+                nc.tensor.transpose(bank[:, 2 + u, :], words[:, u:2 * P:2], ident[:])
+            turned_of[8, 1] = bank
+
         def aside_step(pair, a):
             finish_aside(pair, a, product("c", pair, a))
 
@@ -320,73 +334,70 @@ def tile_plane_product_colour_features_k3_kernel(
             turn_y(pair, 0, 2)
             gather_y(pair, 0, 2, nc.scalar.copy)
 
-        def spread_one(cols32, bias, c, tag="turn", bufs=2):
-            spread_copy(spread_turn(cols32, c, tag, bufs), bias, c)
+        def spread_one(cols, bias, c, tag="turn", bufs=2):
+            spread_copy(spread_turn(cols, c, tag, bufs), bias, c)
 
-        spread_one(u_cols32, u_bias, 0)
-        spread_one(v_cols32, v_bias, 0)
-        spread_one(u_cols32, u_bias, 1, "c0", 1)
-        spread_one(v_cols32, v_bias, 1, "c1", 1)
+        spread_one(u_cols, u_bias, 0)
+        spread_one(v_cols, v_bias, 0)
+        spread_one(u_cols, u_bias, 1, "c0", 1)
+        spread_one(v_cols, v_bias, 1, "c1", 1)
+        spread_one(u_cols, u_bias, 2)
+        spread_one(v_cols, v_bias, 2)
         interleave(nc.vector.tensor_copy, 0, 0, 0, CHUNK)
         quantize_c(0, 0)
         planes_step(0, [])
         piece(0, 1, 0)
         piece(0, 1, 1)
         planes_step(1, [(quantize_c, 0, 1)])
-        spread_one(u_cols32, u_bias, 2)
-        spread_one(v_cols32, v_bias, 2)
         piece(1, 0, 0)
-        basis_step(0, 0)
-        basis_step(0, 1)
-        store_y(0, 0, 2)
         piece(1, 0, 1)
+        planes_step(2, [(quantize_c, 1, 0)], [(basis_step, 0, 0), (basis_step, 0, 1), (store_y, 0, 0, 2)])
         round_y(0, 0, 2)
         piece(1, 1, 0)
-        planes_step(2, [(quantize_c, 1, 0)])
         basis_step(1, 0)
         basis_step(1, 1)
         store_y(1, 0, 2)
+        turn_step(0)
         piece(1, 1, 1)
         round_y(1, 0, 2)
-        planes_step(3, [(quantize_c, 1, 1)])
+        planes_step(3, [(quantize_c, 1, 1), (quantize_y, 0, 2)])
         basis_step(2, 0)
         basis_step(2, 1)
         store_y(2, 0, 2)
         piece(2, 0, 0)
-        turn_step(0)
-        turn_step(1)
         round_y(2, 0, 2)
         piece(2, 0, 1)
-        planes_step(4, [(quantize_y, 0, 4)])
+        planes_step(4, [])
         basis_step(3, 0)
         basis_step(3, 1)
         store_y(3, 0, 2)
+        turn_step(1)
+        turn_step(2)
         piece(2, 1, 0)
         round_y(3, 0, 2)
         piece(2, 1, 1)
-        planes_step(5, [(quantize_c, 2, 0)])
+        planes_step(5, [(quantize_c, 2, 0), (quantize_y, 2, 4)])
+        store_codes(0, 0, T)
+        store_scales(0, 1, [nc.sync])
         basis_step(4, 0)
         basis_step(4, 1)
         store_y(4, 0, 2)
-        turn_step(2)
-        turn_step(3)
         round_y(4, 0, 2)
-        planes_step(6, [(quantize_c, 2, 1), (quantize_y, 4, 4)])
-        store_codes(0, 0, T)
-        store_scales(0, 1, [nc.sync])
-        store_codes(1, 0, PAIR)
+        planes_step(6, [(quantize_c, 2, 1)])
         basis_step(5, 0)
         basis_step(5, 1)
         store_y(5, 0, 2)
+        turn_step(3)
+        turn_step(4)
         round_y(5, 0, 2)
-        planes_step(7, [])
+        planes_step(7, [(quantize_y, 6, 4)])
+        store_codes(1, 0, 2 * PAIR)
         basis_step(6, 0)
         basis_step(6, 1)
         store_y(6, 0, 2)
-        turn_step(4)
-        turn_step(5)
         round_y(6, 0, 2)
         planes_step(8, [])
+        turn_step(5)
         turn_step(6)
         basis_step(7, 0)
         basis_step(7, 1)
@@ -394,20 +405,19 @@ def tile_plane_product_colour_features_k3_kernel(
         round_y(7, 0, 2)
         basis_step(8, 0)
         store_y(8, 0, 1)
-        basis_step(8, 1)
+        last_tile()
         store_y(8, 1, 2)
         round_y(8, 0, 1)
         turn_y(7, 0, 2)
-        gather_y(7, 0, 2, nc.vector.tensor_copy)
+        gather_y(7, 0, 2, nc.scalar.copy)
         turn_y(8, 0, 1)
-        round_y(8, 1, 2)
+        turn_last()
         gather_y(8, 0, 1, nc.scalar.copy)
-        turn_y(8, 1, 2, "c0", 1)
         gather_y(8, 1, 2, nc.scalar.copy)
-        quantize_y(8, 4)
-        store_codes(1, PAIR, T)
-        quantize_y(12, 4)
-        store_codes(2, 0, 2 * PAIR)
+        quantize_y(10, 4)
+        store_codes(1, 2 * PAIR, T)
+        store_codes(2, 0, PAIR)
+        quantize_y(14, 2)
         quantize_y(16, 2)
-        store_codes(2, 2 * PAIR, T)
+        store_codes(2, PAIR, T)
         store_scales(1, 3, [nc.scalar])

from contextlib import ExitStack

import concourse.mybir as mybir
from concourse.masks import make_identity

T, K, F = 768, 1024, 1536
FLOPS = 3 * 2 * T * K * F

F32 = mybir.dt.float32
BF16 = mybir.dt.bfloat16
I32 = mybir.dt.int32
U32 = mybir.dt.uint32
U8 = mybir.dt.uint8
FP8X4 = mybir.dt.float8_e4m3fn_x4
FP4X4 = mybir.dt.float4_e2m1fn_x4
ADD = mybir.AluOpType.add
MULT = mybir.AluOpType.mult

P = 128
PASSES = 2
CHUNK = 512
CHUNKS = 3
PAIR = 256
PAIRS_PER_CHUNK = 3
PAIRS = CHUNKS * PAIRS_PER_CHUNK
HALF = 256


def tile_plane_product_colour_features_k3_kernel(
    tc, x_words, x_scales, u_words, u_scales, v_words, v_scales, colour, u_base, v_base, out_0, out_1, out_2
):
    nc = tc.nc
    with ExitStack() as ctx:
        keep = ctx.enter_context(tc.tile_pool(name="keep", bufs=1))
        work = ctx.enter_context(tc.tile_pool(name="work", bufs=3))
        psum = ctx.enter_context(tc.psum_pool(name="psum", bufs=1))
        ctx.enter_context(tc.manual_schedule())

        ident = keep.tile([P, P], F32, name="ident", align_bytes=64)
        x_codes = keep.tile([P, PAIRS_PER_CHUNK, PASSES, PAIR], U32, name="x_codes", align_bytes=256)
        x_plane = keep.tile([P, PASSES, T], U8, name="x_plane", align_bytes=256)
        u_plane_head = keep.tile([P, PASSES, CHUNK], U8, name="u_plane_head", align_bytes=256)
        u_plane_rest = keep.tile([P, PASSES, F - CHUNK], U8, name="u_plane_rest", align_bytes=256)
        v_plane = keep.tile([P, F], U8, name="v_plane", align_bytes=256)
        u_codes = keep.tile([P, CHUNKS, PASSES, 2 * CHUNK], U8, name="u_codes", align_bytes=256)
        v_codes = keep.tile([P, CHUNKS, PASSES, CHUNK], U32, name="v_codes", align_bytes=256)
        c_rows = keep.tile([P, CHUNKS, PASSES, 4, CHUNK], BF16, name="c_rows", align_bytes=256)
        c_quads = keep.tile([P, CHUNKS, PASSES, CHUNK * 4], BF16, name="c_quads", align_bytes=256)
        c_codes = keep.tile([P, CHUNKS, PASSES, CHUNK], U32, name="c_codes", align_bytes=256)
        c_plane = keep.tile([P, CHUNKS, PASSES, CHUNK], U8, name="c_plane", align_bytes=256)
        u_cols = keep.tile([P, 16], BF16, name="u_cols", align_bytes=64)
        v_cols = keep.tile([P, 16], BF16, name="v_cols", align_bytes=64)
        ident_bf = keep.tile([P, P], BF16, name="ident_bf", align_bytes=64)
        u_bias = keep.tile([P, F], BF16, name="u_bias", align_bytes=64)
        v_bias = keep.tile([P, F], BF16, name="v_bias", align_bytes=64)
        y_codes = keep.tile([P, CHUNKS, T], U32, name="y_codes", align_bytes=256)
        y_plane = keep.tile([P, CHUNKS, T], U8, name="y_plane", align_bytes=256)

        def load_x(pair):
            nc.sync.dma_start(
                out=x_codes[:, pair, :, :].bitcast(I32),
                in_=x_words.rearrange("g p n t -> p g (n t)")[:, :, 4 * pair * PAIR:4 * (pair + 1) * PAIR].bitcast(I32),
            )

        def load_u(c):
            nc.sync.dma_start(
                out=u_codes[:, c, :, :].bitcast(I32),
                in_=u_words.rearrange("g p b -> p g b")[:, :, 2 * c * CHUNK:2 * (c + 1) * CHUNK].bitcast(I32),
            )

        def load_v(c):
            nc.sync.dma_start(
                out=v_codes[:, c, :, :].bitcast(I32),
                in_=v_words.rearrange("g p n t -> p g (n t)")[:, :, 4 * c * CHUNK:4 * (c + 1) * CHUNK].bitcast(I32),
            )

        def load_c(c, g):
            nc.sync.dma_start(
                out=c_rows[:, c, g, :, :],
                in_=colour[512 * g:512 * (g + 1), c * CHUNK:(c + 1) * CHUNK].rearrange("(p j) w -> p j w", j=4),
            )

        def load_cols(queue, cols, base):
            queue.dma_start(
                out=cols[:, 0:12].rearrange("p (c t) -> p c t", t=4),
                in_=base.rearrange("(c p t) -> p c t", p=P, t=4),
            )

        def load_plane(plane, scales, r, lo, hi):
            nc.sync.dma_start(
                out=plane[r:P:32, :, :].bitcast(I32),
                in_=scales[:, r:16:4, lo:hi].rearrange("g q n -> q g n").bitcast(I32),
            )

        def load_v_plane(q, lo, hi):
            nc.sync.dma_start(
                out=v_plane[32 * q + 4:32 * q + 12, lo:hi].bitcast(I32),
                in_=v_scales[:, 4 * q:4 * q + 4, lo:hi].bitcast(I32),
            )

        nc.vector.memset(x_plane[:].rearrange("p g n -> p (g n)").bitcast(I32), 0)
        nc.vector.memset(u_plane_head[:].rearrange("p g n -> p (g n)").bitcast(I32), 0)
        nc.vector.memset(v_plane[:].bitcast(I32), 0)
        nc.vector.memset(u_plane_rest[:].rearrange("p g n -> p (g n)").bitcast(I32), 0)
        make_identity(nc, ident_bf[:])
        make_identity(nc, ident[:])
        load_cols(nc.sync, u_cols, u_base)
        load_cols(nc.sync, v_cols, v_base)
        for r in range(4):
            load_plane(x_plane, x_scales, r, 0, T)
        load_c(0, 0)
        load_x(0)
        for r in range(4):
            load_plane(u_plane_head, u_scales, r, 0, CHUNK)
        load_u(0)
        load_v(0)
        for q in range(4):
            load_v_plane(q, 0, CHUNK)
        load_x(1)
        load_c(0, 1)
        load_x(2)
        load_c(1, 0)
        for r in range(4):
            load_plane(u_plane_rest, u_scales, r, CHUNK, F)
        for q in range(4):
            load_v_plane(q, CHUNK, F)
        load_c(1, 1)
        load_u(1)
        load_v(1)
        load_c(2, 0)
        load_c(2, 1)
        load_u(2)
        load_v(2)


        def spread_turn(cols, c, tag="turn", bufs=2):
            bank = psum.tile([P, 4, P], BF16, name="turn_bank", tag=tag, bufs=bufs)
            for t in range(4):
                nc.tensor.transpose(bank[:, t, :], cols[:, 4 * c + t:4 * c + t + 1].to_broadcast([P, P]), ident_bf[:])
            return bank

        def spread_copy(bank, bias, c):
            nc.scalar.copy(
                out=bias[:, c * CHUNK:(c + 1) * CHUNK].rearrange("q (p t) -> q p t", t=4),
                in_=bank[:].rearrange("q t p -> q p t"),
            )

        def interleave(engine_copy, c, g, lo, hi):
            engine_copy(
                out=c_quads[:, c, g, 4 * lo:4 * hi].rearrange("p (b i t) -> p b t i", i=4, t=4),
                in_=c_rows[:, c, g, :, lo:hi].rearrange("p t (b i) -> p b t i", i=4),
            )

        def quantize_c(c, g):
            nc.vector.quantize_mx(out=c_codes[:, c, g, :].bitcast(FP8X4), scales=c_plane[:, c, g, :], in_=c_quads[:, c, g, :])

        def product(which, pair, a, tag=None):
            c = pair // PAIRS_PER_CHUNK
            t0 = (pair % PAIRS_PER_CHUNK) * PAIR + a * P
            cols = slice(c * CHUNK, (c + 1) * CHUNK)
            bank = psum.tile([P, CHUNK], F32, name="bank", tag=tag or "%s%d" % (which, a))
            for g in range(PASSES):
                if which == "u":
                    rhs = u_codes[:, c, g, :].bitcast(FP4X4)
                    rhs_scale = u_plane_head[:, g, :] if c == 0 else u_plane_rest[:, g, (c - 1) * CHUNK:c * CHUNK]
                elif which == "v":
                    rhs, rhs_scale = v_codes[:, c, g, :].bitcast(FP8X4), v_plane[4 * (g + 1):P, cols]
                else:
                    rhs, rhs_scale = c_codes[:, c, g, :].bitcast(FP8X4), c_plane[:, c, g, :]
                nc.tensor.matmul_mx(
                    out=bank[:],
                    lhsT=x_codes[:, pair % PAIRS_PER_CHUNK, g, a * P:(a + 1) * P].bitcast(FP8X4),
                    lhsT_scale=x_plane[:, g, t0:t0 + P],
                    rhs=rhs,
                    rhs_scale=rhs_scale,
                    start=(g == 0),
                    stop=(g == PASSES - 1),
                )
            return bank

        def add_bias(dst, bank, bias, pair):
            c = pair // PAIRS_PER_CHUNK
            nc.vector.tensor_tensor(out=dst, in0=bank[:], in1=bias[:, c * CHUNK:(c + 1) * CHUNK], op=ADD)

        yb_last = keep.tile([P, CHUNK], BF16, name="yb_last", align_bytes=64)
        planes_of = {}
        y_of = {}
        yb_of = {}
        turned_of = {}
        y_quads = keep.tile([P, PAIRS, 4 * PAIR], BF16, name="y_quads", align_bytes=64)

        def y_tile(pair):
            if pair not in y_of:
                y_of[pair] = work.tile([P, 2, CHUNK], F32, name="y", bufs=4)
            return y_of[pair]

        def finish(pair, a, bank):
            nc.vector.tensor_tensor(out=y_tile(pair)[:, a, :], in0=bank[:], in1=planes_of[pair][:, a, :], op=MULT)

        def finish_aside(pair, a, bank):
            basis = work.tile([P, CHUNK], F32, name="basis")
            nc.scalar.copy(out=basis[:], in_=bank[:])
            nc.gpsimd.tensor_tensor(out=y_tile(pair)[:, a, :], in0=basis[:], in1=planes_of[pair][:, a, :], op=MULT)

        def store_y(pair, lo, hi):
            c = pair // PAIRS_PER_CHUNK
            t0 = (pair % PAIRS_PER_CHUNK) * PAIR
            nc.sync.dma_start(
                out=out_0[t0 + lo * P:t0 + hi * P, c * CHUNK:(c + 1) * CHUNK].rearrange("(a p) f -> p a f", p=P),
                in_=y_of[pair][:, lo:hi, :],
            )

        def round_y(pair, lo, hi):
            if pair not in yb_of:
                yb_of[pair] = work.tile([P, 2, CHUNK], BF16, name="y_bf", align_bytes=64)
            for a in range(lo, hi):
                nc.scalar.copy(
                    out=yb_of[pair][:, a, :].rearrange("m (u p e) -> m u p e", u=2, e=2),
                    in_=y_of[pair][:, a, :].rearrange("m (p u e) -> m u p e", u=2, e=2),
                )

        def turn_y(pair, lo, hi, tag="turn", bufs=2):
            bank = psum.tile([P, 4, P], F32, name="turn_bank", tag=tag, bufs=bufs)
            words = yb_of[pair][:].rearrange("m a f -> m (a f)").bitcast(F32)
            for s in range(2 * lo, 2 * hi):
                nc.tensor.transpose(bank[:, s, :], words[:, s * P:(s + 1) * P], ident[:])
            turned_of[pair, lo] = bank

        def gather_y(pair, lo, hi, engine_copy):
            engine_copy(
                out=y_quads[:, pair, :].bitcast(F32).rearrange("p (a m u) -> p a m u", a=2, u=2)[:, lo:hi],
                in_=turned_of[pair, lo][:].rearrange("p (a u) m -> p a m u", a=2)[:, lo:hi],
            )

        def quantize_y(tile0, tiles):
            lo, hi = tile0 * P, (tile0 + tiles) * P
            nc.vector.quantize_mx(
                out=y_codes[:].rearrange("p c t -> p (c t)")[:, lo:hi].bitcast(FP8X4),
                scales=y_plane[:].rearrange("p c t -> p (c t)")[:, lo:hi],
                in_=y_quads[:].rearrange("p s w -> p (s w)")[:, 4 * lo:4 * hi],
            )

        def store_codes(c, lo, hi):
            nc.sync.dma_start(
                out=out_1[c].rearrange("p m t -> p (m t)")[:, 4 * lo:4 * hi].bitcast(I32),
                in_=y_codes[:, c, lo:hi].bitcast(I32),
            )

        def store_scales(lo, hi, queues):
            for q in range(4):
                queues[q % len(queues)].dma_start(
                    out=out_2[lo:hi, 4 * q:4 * q + 4, :].rearrange("g r n -> r g n").bitcast(I32),
                    in_=y_plane[32 * q:32 * q + 4, lo:hi, :].bitcast(I32),
                )

        def spread(c):
            bank_u = spread_turn(u_cols, c)
            bank_v = spread_turn(v_cols, c)
            spread_copy(bank_u, u_bias, c)
            spread_copy(bank_v, v_bias, c)

        def piece(c, g, h):
            interleave(nc.scalar.copy, c, g, h * HALF, (h + 1) * HALF)

        def multiply_planes(pair, lo, hi, first, second):
            nc.gpsimd.tensor_tensor(
                out=planes_of[pair][:, lo:hi, :], in0=first[:, lo:hi, :], in1=second[:, lo:hi, :], op=MULT
            )

        state = {}

        def planes_step(pair, quantize_now, between=()):
            first = work.tile([P, 2, CHUNK], F32, name="first")
            second = work.tile([P, 2, CHUNK], F32, name="second")
            planes_of[pair] = work.tile([P, 2, CHUNK], F32, name="planes", bufs=4)
            if pair == 0:
                ua = product("u", pair, 0)
                ub = product("u", pair, 1)
                va = product("v", pair, 0)
                vb = product("v", pair, 1)
                add_bias(first[:, 0, :], ua, u_bias, pair)
                add_bias(first[:, 1, :], ub, u_bias, pair)
                add_bias(second[:, 0, :], va, v_bias, pair)
                multiply_planes(pair, 0, 1, first, second)
            else:
                ua = product("u", pair, 0)
                va = product("v", pair, 0)
                add_bias(first[:, 0, :], ua, u_bias, pair)
                if pair == PAIRS - 1:
                    for step in quantize_now:
                        step[0](*step[1:])
                    quantize_now = []
                add_bias(second[:, 0, :], va, v_bias, pair)
                if pair == PAIRS - 1:
                    multiply_planes(pair, 0, 1, first, second)
                for step in between:
                    step[0](*step[1:])
                ub = product("u", pair, 1)
                vb = product("v", pair, 1)
                add_bias(first[:, 1, :], ub, u_bias, pair)
            for step in quantize_now:
                step[0](*step[1:])
            if pair == 0:
                add_bias(second[:, 1, :], vb, v_bias, pair)
            else:
                add_bias(second[:, 1, :], vb, v_bias, pair)
            multiply_planes(pair, 1 if pair in (0, PAIRS - 1) else 0, 2, first, second)

        def basis_step(pair, a):
            finish(pair, a, product("c", pair, a, ("u0", "v0")[a] if pair == PAIRS - 1 else None))

        def basis_pair(pair):
            ca = product("c", pair, 0)
            cb = product("c", pair, 1)
            finish(pair, 1, cb)
            finish(pair, 0, ca)

        def last_tile():
            bank = product("c", 8, 1, "v0")
            nc.vector.tensor_tensor(out=yb_last[:], in0=bank[:], in1=planes_of[8][:, 1, :], op=MULT)
            finish(8, 1, bank)

        def turn_last():
            bank = psum.tile([P, 4, P], F32, name="turn_bank", tag="c0", bufs=1)
            words = yb_last[:].bitcast(F32)
            for u in range(2):
                nc.tensor.transpose(bank[:, 2 + u, :], words[:, u:2 * P:2], ident[:])
            turned_of[8, 1] = bank

        def aside_step(pair, a):
            finish_aside(pair, a, product("c", pair, a))

        def turn_step(pair):
            turn_y(pair, 0, 2)
            gather_y(pair, 0, 2, nc.scalar.copy)

        def spread_one(cols, bias, c, tag="turn", bufs=2):
            spread_copy(spread_turn(cols, c, tag, bufs), bias, c)

        spread_one(u_cols, u_bias, 0)
        spread_one(v_cols, v_bias, 0)
        spread_one(u_cols, u_bias, 1, "c0", 1)
        spread_one(v_cols, v_bias, 1, "c1", 1)
        spread_one(u_cols, u_bias, 2)
        spread_one(v_cols, v_bias, 2)
        interleave(nc.vector.tensor_copy, 0, 0, 0, CHUNK)
        quantize_c(0, 0)
        planes_step(0, [])
        piece(0, 1, 0)
        piece(0, 1, 1)
        planes_step(1, [(quantize_c, 0, 1)])
        piece(1, 0, 0)
        piece(1, 0, 1)
        planes_step(2, [(quantize_c, 1, 0)], [(basis_step, 0, 0), (basis_step, 0, 1), (store_y, 0, 0, 2)])
        round_y(0, 0, 2)
        piece(1, 1, 0)
        basis_step(1, 0)
        basis_step(1, 1)
        store_y(1, 0, 2)
        turn_step(0)
        piece(1, 1, 1)
        round_y(1, 0, 2)
        planes_step(3, [(quantize_c, 1, 1), (quantize_y, 0, 2)])
        basis_step(2, 0)
        basis_step(2, 1)
        store_y(2, 0, 2)
        piece(2, 0, 0)
        round_y(2, 0, 2)
        piece(2, 0, 1)
        planes_step(4, [])
        basis_step(3, 0)
        basis_step(3, 1)
        store_y(3, 0, 2)
        turn_step(1)
        turn_step(2)
        piece(2, 1, 0)
        round_y(3, 0, 2)
        piece(2, 1, 1)
        planes_step(5, [(quantize_c, 2, 0), (quantize_y, 2, 4)])
        store_codes(0, 0, T)
        store_scales(0, 1, [nc.sync])
        basis_step(4, 0)
        basis_step(4, 1)
        store_y(4, 0, 2)
        round_y(4, 0, 2)
        planes_step(6, [(quantize_c, 2, 1)])
        basis_step(5, 0)
        basis_step(5, 1)
        store_y(5, 0, 2)
        turn_step(3)
        turn_step(4)
        round_y(5, 0, 2)
        planes_step(7, [(quantize_y, 6, 4)])
        store_codes(1, 0, 2 * PAIR)
        basis_step(6, 0)
        basis_step(6, 1)
        store_y(6, 0, 2)
        round_y(6, 0, 2)
        planes_step(8, [])
        turn_step(5)
        turn_step(6)
        basis_step(7, 0)
        basis_step(7, 1)
        store_y(7, 0, 2)
        round_y(7, 0, 2)
        basis_step(8, 0)
        store_y(8, 0, 1)
        last_tile()
        store_y(8, 1, 2)
        round_y(8, 0, 1)
        turn_y(7, 0, 2)
        gather_y(7, 0, 2, nc.scalar.copy)
        turn_y(8, 0, 1)
        turn_last()
        gather_y(8, 0, 1, nc.scalar.copy)
        gather_y(8, 1, 2, nc.scalar.copy)
        quantize_y(10, 4)
        store_codes(1, 2 * PAIR, T)
        store_codes(2, 0, PAIR)
        quantize_y(14, 2)
        quantize_y(16, 2)
        store_codes(2, PAIR, T)
        store_scales(1, 3, [nc.scalar])
